import numpy as np
import ml_dtypes


def mxq(x, axis, fmt="e4m3"):
    dtype, down = {"e4m3": (ml_dtypes.float8_e4m3fn, 7), "e5m2": (ml_dtypes.float8_e5m2, 14)}[fmt]
    v = np.moveaxis(np.asarray(x, np.float32).astype(ml_dtypes.bfloat16).astype(np.float64), axis, -1)
    blocks = v.reshape(v.shape[:-1] + (-1, 32))
    amax = np.abs(blocks).max(-1, keepdims=True)
    byte = np.maximum(np.where(amax > 0, np.frexp(amax)[1] - 1 + 127, 0) - down, 1)
    scale = np.exp2(byte - 127.0)
    codes = (blocks / scale).astype(np.float32).astype(dtype).astype(np.float64)
    return np.moveaxis((codes * scale).reshape(v.shape), -1, axis)


WIDE = False


def mx_kscale(k):
    if not WIDE:
        return np.ones(k)
    levels = np.array([10, -10, 5, -5, 0])
    if k % 512:
        return np.exp2(np.random.permutation(np.resize(levels, k // 32))).repeat(32)
    a = np.empty((k // 512, 16))
    for p in range(k // 512):
        a[p, :8] = np.random.permutation(np.resize(levels, 8))
        for g in range(8):
            far = levels[np.abs(levels - a[p, g]) >= 10]
            a[p, g + 8] = far[np.random.randint(len(far))]
    return np.exp2(a.ravel()).repeat(32)


def f64(x):
    return np.asarray(x).astype(np.float64)


def striped(idx):
    return np.tile(np.asarray(idx).reshape(-1, 16).T, (8, 1)).astype(np.uint16)


def unstriped(offs):
    return offs[:16].T.reshape(-1).astype(np.int64)


E2M1 = np.array([0.0, 0.5, 1.0, 1.5, 2.0, 3.0, 4.0, 6.0, -0.0, -0.5, -1.0, -1.5, -2.0, -3.0, -4.0, -6.0])


def pack_weight(w, fmt):
    k, n = w.shape
    w = f64(np.asarray(w, np.float32).astype(ml_dtypes.bfloat16)).reshape(k // 32, 32, n)
    amax = np.abs(w).max(1)
    if fmt == "e4m3":
        byte = np.frexp(amax)[1] - 1 + 127 - 7
    else:
        mant, ex = np.frexp(amax / 6.0)
        byte = np.where(mant > 0.5, ex, ex - 1) + 127
    byte = np.clip(np.where(amax > 0, byte, 1), 1, 254)
    scaled = (w * np.exp2(127.0 - byte)[:, None, :]).reshape(k, n).astype(np.float32)
    by_word = np.ascontiguousarray(scaled.reshape(k // 512, 128, 4, n).transpose(0, 1, 3, 2))
    if fmt == "e4m3":
        words = by_word.astype(ml_dtypes.float8_e4m3fn).view(np.uint8)
    else:
        c = by_word.astype(ml_dtypes.float4_e2m1fn).view(np.uint8) & 0xF
        words = (c[..., 0::2] | (c[..., 1::2] << 4)).reshape(k // 512, 128, 2 * n)
    return np.ascontiguousarray(words), np.ascontiguousarray(byte.astype(np.uint8).reshape(k // 512, 16, n))


def unpack_weight(words, scales, fmt):
    g, _, n = scales.shape
    words = np.ascontiguousarray(words).reshape(g, 128, n, -1)
    if fmt == "e4m3":
        vals = words.view(ml_dtypes.float8_e4m3fn).astype(np.float64)
    else:
        nib = np.empty((g, 128, n, 4), np.uint8)
        nib[..., 0::2] = words & 0xF
        nib[..., 1::2] = words >> 4
        vals = E2M1[nib]
    vals = vals * np.repeat(np.exp2(scales.astype(np.float64) - 127.0), 8, axis=1)[..., None]
    return vals.transpose(0, 1, 3, 2).reshape(g * 512, n)


D, E, T, I, Q, G = 512, 512, 2048, 512, 128, 64


def setup_inputs():
    n = np.random.standard_normal
    idx = np.random.permutation(T)[:I]
    fd = mx_kscale(D)
    fe = mx_kscale(E)
    keysp = pack_weight(n((D, T)) / fd[:, None], "e4m3")
    valsp = pack_weight(n((E, T)) / fe[:, None], "e4m3")
    return {
        "query": (n((D, Q)) * 0.8 / np.sqrt(D) * fd[:, None]).astype(np.float32),
        "query2": (n((D, Q)) * 0.8 / np.sqrt(D) * fd[:, None]).astype(np.float32),
        "keys_words": keysp[0],
        "keys_scales": keysp[1],
        "gout": (n((E, Q)) * 1 / np.sqrt(E) * fe[:, None]).astype(np.float32),
        "vals_words": valsp[0],
        "vals_scales": valsp[1],
        "dquery": (n((D, Q)) * 1.0 / np.sqrt(D) * fd[:, None]).astype(np.float32),
        "base": (0.5 * n((Q, T))).astype(np.float32),
        "offs": striped(idx),
    }


def reference(query, query2, keys_words, keys_scales, gout, vals_words, vals_scales, dquery, base, offs):
    idx = unstriped(offs)
    keysu = unpack_weight(keys_words, keys_scales, "e4m3")
    valsu = unpack_weight(vals_words, vals_scales, "e4m3")
    queryq = mxq(f64(query), 0, "e4m3")
    keysidxg = keysu[:, idx]
    a = queryq.T @ keysidxg
    dqueryq = mxq(f64(dquery), 0, "e4m3")
    ta = dqueryq.T @ keysidxg
    query2q = mxq(f64(query2), 0, "e4m3")
    b = query2q.T @ keysidxg
    pa = np.exp(a)
    sa = pa.reshape(Q, G, I // G).sum(axis=2)
    z = np.sum(sa, axis=1, keepdims=True)
    pb = np.exp(b)
    sb = pb.reshape(Q, G, I // G).sum(axis=2)
    goutq = mxq(f64(gout), 0, "e4m3")
    valsidxg = valsu[:, idx]
    c0 = goutq.T @ valsidxg
    drr = c0 * pb
    dr = drr.reshape(Q, G, I // G).sum(axis=2)
    dz = np.sum(dr / sb * sa / np.square(z) * (-1.0), axis=1, keepdims=True)
    dsa = dr / sb / z + dz
    r1 = np.repeat(dsa, I // G, axis=1)
    tpa = ta * pa
    tsa = tpa.reshape(Q, G, I // G).sum(axis=2)
    tz = np.sum(tsa, axis=1, keepdims=True)
    tdz = np.sum((tsa * dr / sb - tz * z * 2.0 * dr / sb * sa / np.square(z)) / np.square(z) * (-1.0), axis=1, keepdims=True)
    tdsa = tz * dr / sb / np.square(z) * (-1.0) + tdz
    tr1 = np.repeat(tdsa, I // G, axis=1)
    tda = tr1 * pa + tpa * r1
    gs = tda * 512.0
    gf = np.zeros((Q, T))
    gf[:, idx] = gs
    y = f64(base) + gf
    return y

@@ -1,0 +1,179 @@
+from contextlib import ExitStack
+
+import concourse.mybir as mybir
+
+D, T, I, Q, G = 512, 2048, 512, 128, 64
+PAGE = I // G
+P = 128
+PACK = 4
+FLOPS = 4 * 2 * D * Q * I
+
+F32 = mybir.dt.float32
+BF16 = mybir.dt.bfloat16
+I32 = mybir.dt.int32
+U32 = mybir.dt.uint32
+U16 = mybir.dt.uint16
+U8 = mybir.dt.uint8
+FP8X4 = mybir.dt.float8_e4m3fn_x4
+ALU = mybir.AluOpType
+ACT = mybir.ActivationFunctionType
+AX = mybir.AxisListType
+
+KEY_ROW0 = 0
+VAL_ROW0 = 4
+OUT_CHUNKS = (512, 512, 512, 256, 256)
+
+
+def tile_attend_hvpagethensecond_s_kernel(
+    tc, query, query2, keys_words, keys_scales, gout, vals_words, vals_scales, dquery, base, offs, out
+):
+    nc = tc.nc
+    with ExitStack() as ctx:
+        sb = ctx.enter_context(tc.tile_pool(name="sb", bufs=1))
+        ps = ctx.enter_context(tc.psum_pool(name="ps", bufs=1))
+
+        def load_scales(name, scales, row0, queue, tag):
+            tile = sb.tile([P, T], U8, name=name, tag=tag, align_bytes=64)
+            nc.vector.memset(tile[:].bitcast(I32), 0)
+            for quad in range(4):
+                queue.dma_start(
+                    out=tile[32 * quad + row0 : 32 * quad + row0 + 4, :].bitcast(I32),
+                    in_=scales[0, 4 * quad : 4 * quad + 4, :].bitcast(I32),
+                )
+            return tile
+
+        def load_words(name, words, tag):
+            tile = sb.tile([P, T], I32, name=name, tag=tag, align_bytes=64)
+            nc.sync.dma_start(out=tile[:], in_=words[0].rearrange("p n t -> p (n t)").bitcast(I32))
+            return tile
+
+        def load_rows(name, rows):
+            tile = sb.tile([P, PACK, Q], F32, name=name, tag="raw", bufs=2, align_bytes=64)
+            nc.sync.dma_start(out=tile[:], in_=rows.rearrange("(p j) q -> p j q", j=PACK))
+            return tile
+
+        def gather(name, window, dtype):
+            tile = sb.tile([P, I], dtype, name=name, align_bytes=64)
+            nc.vector.tensor_copy(tile[:], window[:].bitcast(dtype).indirect(offsets[:]))
+            return tile
+
+        def quantise(name, raw):
+            grouped = sb.tile([P, Q, PACK], BF16, name=name + "_bf", align_bytes=64)
+            nc.scalar.copy(out=grouped[:], in_=raw[:].rearrange("p j q -> p q j"))
+            codes = sb.tile([P, Q], U32, name=name + "_codes", align_bytes=64)
+            scale = sb.tile([P, Q], U8, name=name + "_scale", align_bytes=64)
+            nc.vector.quantize_mx(
+                out=codes[:].bitcast(FP8X4), scales=scale[:], in_=grouped[:].rearrange("p q j -> p (q j)")
+            )
+            return codes, scale
+
+        def scores(name, rows, words, scale, row0):
+            acc = ps.tile([P, I], F32, name=name)
+            nc.tensor.matmul_mx(
+                out=acc[:],
+                lhsT=rows[0][:].bitcast(FP8X4),
+                lhsT_scale=rows[1][:],
+                rhs=words[:].bitcast(FP8X4),
+                rhs_scale=scale[row0:, :],
+                start=True,
+                stop=True,
+            )
+            return acc
+
+        def column(name):
+            return sb.tile([P, 1], F32, name=name)
+
+        def by_page(ap):
+            return ap.rearrange("p (g j) -> p g j", j=PAGE)
+
+        def spread(tile):
+            return tile[:].unsqueeze(2).to_broadcast([P, G, PAGE])
+
+        offsets = sb.tile([P, I // 16], U16, name="offsets")
+        nc.sync.dma_start(offsets[:], offs)
+        key_words = load_words("key_words", keys_words, "key_words")
+        key_scales = load_scales("key_scales", keys_scales, KEY_ROW0, nc.scalar, "early")
+        q2_raw = load_rows("q2_raw", query2)
+        q1_raw = load_rows("q1_raw", query)
+        val_scales = load_scales("val_scales", vals_scales, VAL_ROW0, nc.sync, "val_scales")
+
+        placed = sb.tile([P, T], F32, name="placed")
+        nc.vector.memset(placed[:], 0.0)
+
+        ks = gather("ks", key_scales, U8)
+        val_words = load_words("val_words", vals_words, "early")
+        kw = gather("kw", key_words, U32)
+        q2 = quantise("q2", q2_raw)
+        go_raw = load_rows("go_raw", gout)
+        q1 = quantise("q1", q1_raw)
+        dq_raw = load_rows("dq_raw", dquery)
+        b = scores("b", q2, kw, ks, KEY_ROW0)
+        a = scores("a", q1, kw, ks, KEY_ROW0)
+        vs = gather("vs", val_scales, U8)
+
+        pb = sb.tile([P, I], F32, name="pb")
+        nc.scalar.activation(out=pb[:], in_=b[:], func=ACT.Exp)
+        pa = sb.tile([P, I], F32, name="pa")
+        z = column("z")
+        nc.scalar.activation(out=pa[:], in_=a[:], func=ACT.Exp, accum_out=z[:])
+
+        vw = gather("vw", val_words, U32)
+        base_sb = sb.tile([P, T], F32, name="base_sb", tag="early", align_bytes=64)
+        nc.sync.dma_start(out=base_sb[:], in_=base)
+        c0 = scores("c0", quantise("go", go_raw), vw, vs, VAL_ROW0)
+        ta = scores("ta", quantise("dq", dq_raw), kw, ks, KEY_ROW0)
+
+        sbp = sb.tile([P, G], F32, name="sbp")
+        nc.vector.tensor_reduce(out=sbp[:], in_=by_page(pb[:]), axis=AX.X, op=ALU.add)
+        rz = column("rz")
+        nc.vector.reciprocal(out=rz[:], in_=z[:])
+        rsb = sb.tile([P, G], F32, name="rsb")
+        nc.vector.reciprocal(out=rsb[:], in_=sbp[:])
+        rz512 = column("rz512")
+        nc.scalar.mul(rz512[:], rz[:], 512.0)
+        nrz = column("nrz")
+        nc.scalar.mul(nrz[:], rz[:], -1.0)
+
+        drr = sb.tile([P, I], F32, name="drr")
+        nc.vector.tensor_tensor(out=drr[:], in0=c0[:], in1=pb[:], op=ALU.mult)
+        junk = sb.tile([P, I], F32, name="junk")
+        m = column("m")
+        nc.vector.scalar_tensor_tensor(
+            out=junk[:], in0=ta[:], scalar=rz[:], in1=pa[:], op0=ALU.mult, op1=ALU.mult, accum_out=m[:]
+        )
+        dr = sb.tile([P, G], F32, name="dr")
+        nc.vector.tensor_reduce(out=dr[:], in_=by_page(drr[:]), axis=AX.X, op=ALU.add)
+        e = sb.tile([P, I], F32, name="e")
+        nc.vector.scalar_tensor_tensor(
+            out=e[:], in0=ta[:], scalar=m[:], in1=pa[:], op0=ALU.subtract, op1=ALU.mult
+        )
+        u = sb.tile([P, G], F32, name="u")
+        nc.vector.scalar_tensor_tensor(
+            out=u[:], in0=dr[:], scalar=rz512[:], in1=rsb[:], op0=ALU.mult, op1=ALU.mult
+        )
+        junk2 = sb.tile([P, I], F32, name="junk2")
+        ubar = column("ubar")
+        nc.vector.scalar_tensor_tensor(
+            out=by_page(junk2[:]), in0=spread(u), scalar=rz[:], in1=by_page(pa[:]),
+            op0=ALU.mult, op1=ALU.mult, accum_out=ubar[:],
+        )
+        x = sb.tile([P, I], F32, name="x")
+        cz = column("cz")
+        nc.vector.scalar_tensor_tensor(
+            out=by_page(x[:]), in0=spread(u), scalar=ubar[:], in1=by_page(e[:]),
+            op0=ALU.subtract, op1=ALU.mult, accum_out=cz[:],
+        )
+        y = sb.tile([P, I], F32, name="y")
+        nc.vector.tensor_scalar(
+            out=y[:], in0=pa[:], scalar1=cz[:], scalar2=nrz[:], op0=ALU.mult, op1=ALU.mult
+        )
+        nc.vector.tensor_tensor(placed[:].indirect(offsets[:]), x[:], y[:], ALU.add)
+
+        start = 0
+        for n, width in enumerate(OUT_CHUNKS):
+            cols = slice(start, start + width)
+            res = sb.tile([P, width], F32, name="res%d" % n)
+            nc.vector.tensor_tensor(out=res[:], in0=placed[:, cols], in1=base_sb[:, cols], op=ALU.add)
+            queue = nc.sync if n % 2 == 0 else nc.scalar
+            queue.dma_start(out=out[:, cols], in_=res[:])
+            start = start + width

@@ -21,7 +21,7 @@ AX = mybir.AxisListType
 
 KEY_ROW0 = 0
 VAL_ROW0 = 4
-OUT_CHUNKS = (512, 512, 512, 256, 256)
+OUT_CHUNKS = (384, 384, 384, 384, 256, 256)
 
 
 def tile_attend_hvpagethensecond_s_kernel(
@@ -58,7 +58,7 @@ def tile_attend_hvpagethensecond_s_kernel(
             return tile
 
         def quantise(name, raw):
-            grouped = sb.tile([P, Q, PACK], BF16, name=name + "_bf", align_bytes=64)
+            grouped = sb.tile([P, Q, PACK], BF16, name=name + "_bf", tag=name + "_bf", align_bytes=64)
             nc.scalar.copy(out=grouped[:], in_=raw[:].rearrange("p j q -> p q j"))
             codes = sb.tile([P, Q], U32, name=name + "_codes", align_bytes=64)
             scale = sb.tile([P, Q], U8, name=name + "_scale", align_bytes=64)
@@ -92,16 +92,16 @@ def tile_attend_hvpagethensecond_s_kernel(
         offsets = sb.tile([P, I // 16], U16, name="offsets")
         nc.sync.dma_start(offsets[:], offs)
         key_words = load_words("key_words", keys_words, "key_words")
-        key_scales = load_scales("key_scales", keys_scales, KEY_ROW0, nc.scalar, "early")
+        key_scales = load_scales("key_scales", keys_scales, KEY_ROW0, nc.scalar, "key_scales")
         q2_raw = load_rows("q2_raw", query2)
         q1_raw = load_rows("q1_raw", query)
+        val_words = load_words("val_words", vals_words, "val_words")
         val_scales = load_scales("val_scales", vals_scales, VAL_ROW0, nc.sync, "val_scales")
 
         placed = sb.tile([P, T], F32, name="placed")
         nc.vector.memset(placed[:], 0.0)
 
         ks = gather("ks", key_scales, U8)
-        val_words = load_words("val_words", vals_words, "early")
         kw = gather("kw", key_words, U32)
         q2 = quantise("q2", q2_raw)
         go_raw = load_rows("go_raw", gout)
@@ -109,7 +109,6 @@ def tile_attend_hvpagethensecond_s_kernel(
         dq_raw = load_rows("dq_raw", dquery)
         b = scores("b", q2, kw, ks, KEY_ROW0)
         a = scores("a", q1, kw, ks, KEY_ROW0)
-        vs = gather("vs", val_scales, U8)
 
         pb = sb.tile([P, I], F32, name="pb")
         nc.scalar.activation(out=pb[:], in_=b[:], func=ACT.Exp)
@@ -118,28 +117,30 @@ def tile_attend_hvpagethensecond_s_kernel(
         nc.scalar.activation(out=pa[:], in_=a[:], func=ACT.Exp, accum_out=z[:])
 
         vw = gather("vw", val_words, U32)
-        base_sb = sb.tile([P, T], F32, name="base_sb", tag="early", align_bytes=64)
+        base_sb = sb.tile([P, T], F32, name="base_sb", tag="val_words", align_bytes=64)
         nc.sync.dma_start(out=base_sb[:], in_=base)
+        vs = gather("vs", val_scales, U8)
         c0 = scores("c0", quantise("go", go_raw), vw, vs, VAL_ROW0)
         ta = scores("ta", quantise("dq", dq_raw), kw, ks, KEY_ROW0)
 
-        sbp = sb.tile([P, G], F32, name="sbp")
-        nc.vector.tensor_reduce(out=sbp[:], in_=by_page(pb[:]), axis=AX.X, op=ALU.add)
-        rz = column("rz")
-        nc.vector.reciprocal(out=rz[:], in_=z[:])
+        stats = sb.tile([P, G + 1], F32, name="stats", tag="go_bf", align_bytes=64)
+        sbp = stats[:, 0:G]
+        rz = stats[:, G : G + 1]
+        nc.vector.tensor_reduce(out=sbp, in_=by_page(pb[:]), axis=AX.X, op=ALU.add)
+        nc.vector.reciprocal(out=rz, in_=z[:])
+        root = sb.tile([P, G], F32, name="root")
+        nc.scalar.activation(out=root[:], in_=sbp, func=ACT.Abs_reciprocal_sqrt, scale=1.0 / 512.0)
         rsb = sb.tile([P, G], F32, name="rsb")
-        nc.vector.reciprocal(out=rsb[:], in_=sbp[:])
-        rz512 = column("rz512")
-        nc.scalar.mul(rz512[:], rz[:], 512.0)
+        nc.scalar.activation(out=rsb[:], in_=root[:], func=ACT.Square)
         nrz = column("nrz")
-        nc.scalar.mul(nrz[:], rz[:], -1.0)
+        nc.scalar.mul(nrz[:], rz, -1.0)
 
         drr = sb.tile([P, I], F32, name="drr")
         nc.vector.tensor_tensor(out=drr[:], in0=c0[:], in1=pb[:], op=ALU.mult)
         junk = sb.tile([P, I], F32, name="junk")
         m = column("m")
         nc.vector.scalar_tensor_tensor(
-            out=junk[:], in0=ta[:], scalar=rz[:], in1=pa[:], op0=ALU.mult, op1=ALU.mult, accum_out=m[:]
+            out=junk[:], in0=ta[:], scalar=rz, in1=pa[:], op0=ALU.mult, op1=ALU.mult, accum_out=m[:]
         )
         dr = sb.tile([P, G], F32, name="dr")
         nc.vector.tensor_reduce(out=dr[:], in_=by_page(drr[:]), axis=AX.X, op=ALU.add)
@@ -149,12 +150,12 @@ def tile_attend_hvpagethensecond_s_kernel(
         )
         u = sb.tile([P, G], F32, name="u")
         nc.vector.scalar_tensor_tensor(
-            out=u[:], in0=dr[:], scalar=rz512[:], in1=rsb[:], op0=ALU.mult, op1=ALU.mult
+            out=u[:], in0=dr[:], scalar=rz, in1=rsb[:], op0=ALU.mult, op1=ALU.mult
         )
         junk2 = sb.tile([P, I], F32, name="junk2")
         ubar = column("ubar")
         nc.vector.scalar_tensor_tensor(
-            out=by_page(junk2[:]), in0=spread(u), scalar=rz[:], in1=by_page(pa[:]),
+            out=by_page(junk2[:]), in0=spread(u), scalar=rz, in1=by_page(pa[:]),
             op0=ALU.mult, op1=ALU.mult, accum_out=ubar[:],
         )
         x = sb.tile([P, I], F32, name="x")

@@ -35,10 +35,10 @@ def tile_attend_hvpagethensecond_s_kernel(
         def load_scales(name, scales, row0, queue, tag):
             tile = sb.tile([P, T], U8, name=name, tag=tag, align_bytes=64)
             nc.vector.memset(tile[:].bitcast(I32), 0)
-            for quad in range(4):
+            for row in range(4):
                 queue.dma_start(
-                    out=tile[32 * quad + row0 : 32 * quad + row0 + 4, :].bitcast(I32),
-                    in_=scales[0, 4 * quad : 4 * quad + 4, :].bitcast(I32),
+                    out=tile[row0 + row : P : 32, :].bitcast(I32),
+                    in_=scales[0, row:16:4, :].bitcast(I32),
                 )
             return tile
 
@@ -59,7 +59,10 @@ def tile_attend_hvpagethensecond_s_kernel(
 
         def quantise(name, raw):
             grouped = sb.tile([P, Q, PACK], BF16, name=name + "_bf", tag=name + "_bf", align_bytes=64)
-            nc.scalar.copy(out=grouped[:], in_=raw[:].rearrange("p j q -> p q j"))
+            nc.scalar.copy(
+                out=grouped[:].rearrange("p (c i) j -> p c j i", i=4),
+                in_=raw[:].rearrange("p j (c i) -> p c j i", i=4),
+            )
             codes = sb.tile([P, Q], U32, name=name + "_codes", align_bytes=64)
             scale = sb.tile([P, Q], U8, name=name + "_scale", align_bytes=64)
             nc.vector.quantize_mx(

@@ -138,29 +138,48 @@ def tile_attend_hvpagethensecond_s_kernel(
         nrz = column("nrz")
         nc.scalar.mul(nrz[:], rz, -1.0)
 
+
+        quads = sb.tile([P, G, 4], F32, name="quads", tag="dq_bf", align_bytes=64)
+        nc.gpsimd.tensor_tensor(out=quads[:], in0=by_page(pa[:])[:, :, 0:4], in1=by_page(pa[:])[:, :, 4:8], op=ALU.add)
+        pairs = sb.tile([P, G, 2], F32, name="pairs")
+        nc.gpsimd.tensor_tensor(out=pairs[:], in0=quads[:, :, 0:2], in1=quads[:, :, 2:4], op=ALU.add)
+        pairs_n = sb.tile([P, G, 2], F32, name="pairs_n")
+        nc.gpsimd.tensor_scalar(
+            out=pairs_n[:], in0=pairs[:], scalar1=rz, scalar2=0.0, op0=ALU.mult, op1=ALU.add
+        )
+        share = sb.tile([P, G, 2], F32, name="share")
+        nc.gpsimd.tensor_tensor(
+            out=share[:], in0=pairs_n[:], in1=rsb[:].unsqueeze(2).to_broadcast([P, G, 2]), op=ALU.mult
+        )
+
         drr = sb.tile([P, I], F32, name="drr")
         nc.vector.tensor_tensor(out=drr[:], in0=c0[:], in1=pb[:], op=ALU.mult)
         junk = sb.tile([P, I], F32, name="junk")
         m = column("m")
         nc.vector.scalar_tensor_tensor(
-            out=junk[:], in0=ta[:], scalar=rz, in1=pa[:], op0=ALU.mult, op1=ALU.mult, accum_out=m[:]
+            out=junk[:], in0=pa[:], scalar=rz, in1=ta[:], op0=ALU.mult, op1=ALU.mult, accum_out=m[:]
         )
         dr = sb.tile([P, G], F32, name="dr")
         nc.vector.tensor_reduce(out=dr[:], in_=by_page(drr[:]), axis=AX.X, op=ALU.add)
         e = sb.tile([P, I], F32, name="e")
-        nc.vector.scalar_tensor_tensor(
-            out=e[:], in0=ta[:], scalar=m[:], in1=pa[:], op0=ALU.subtract, op1=ALU.mult
-        )
+
+        def centred(cols):
+            nc.vector.scalar_tensor_tensor(
+                out=e[:, cols], in0=ta[:, cols], scalar=m[:], in1=pa[:, cols], op0=ALU.subtract, op1=ALU.mult
+            )
+
+        centred(slice(0, I // 2))
         u = sb.tile([P, G], F32, name="u")
         nc.vector.scalar_tensor_tensor(
             out=u[:], in0=dr[:], scalar=rz, in1=rsb[:], op0=ALU.mult, op1=ALU.mult
         )
-        junk2 = sb.tile([P, I], F32, name="junk2")
+        junk2 = sb.tile([P, G, 2], F32, name="junk2")
         ubar = column("ubar")
         nc.vector.scalar_tensor_tensor(
-            out=by_page(junk2[:]), in0=spread(u), scalar=rz, in1=by_page(pa[:]),
+            out=junk2[:], in0=dr[:].unsqueeze(2).to_broadcast([P, G, 2]), scalar=rz, in1=share[:],
             op0=ALU.mult, op1=ALU.mult, accum_out=ubar[:],
         )
+        centred(slice(I // 2, I))
         x = sb.tile([P, I], F32, name="x")
         cz = column("cz")
         nc.vector.scalar_tensor_tensor(

from contextlib import ExitStack

import concourse.mybir as mybir

D, T, I, Q, G = 512, 2048, 512, 128, 64
PAGE = I // G
P = 128
PACK = 4
FLOPS = 4 * 2 * D * Q * I

F32 = mybir.dt.float32
BF16 = mybir.dt.bfloat16
I32 = mybir.dt.int32
U32 = mybir.dt.uint32
U16 = mybir.dt.uint16
U8 = mybir.dt.uint8
FP8X4 = mybir.dt.float8_e4m3fn_x4
ALU = mybir.AluOpType
ACT = mybir.ActivationFunctionType
AX = mybir.AxisListType

KEY_ROW0 = 0
VAL_ROW0 = 4
OUT_CHUNKS = (384, 384, 384, 384, 256, 256)


def tile_attend_hvpagethensecond_s_kernel(
    tc, query, query2, keys_words, keys_scales, gout, vals_words, vals_scales, dquery, base, offs, out
):
    nc = tc.nc
    with ExitStack() as ctx:
        sb = ctx.enter_context(tc.tile_pool(name="sb", bufs=1))
        ps = ctx.enter_context(tc.psum_pool(name="ps", bufs=1))

        def load_scales(name, scales, row0, queue, tag):
            tile = sb.tile([P, T], U8, name=name, tag=tag, align_bytes=64)
            nc.vector.memset(tile[:].bitcast(I32), 0)
            for row in range(4):
                queue.dma_start(
                    out=tile[row0 + row : P : 32, :].bitcast(I32),
                    in_=scales[0, row:16:4, :].bitcast(I32),
                )
            return tile

        def load_words(name, words, tag):
            tile = sb.tile([P, T], I32, name=name, tag=tag, align_bytes=64)
            nc.sync.dma_start(out=tile[:], in_=words[0].rearrange("p n t -> p (n t)").bitcast(I32))
            return tile

        def load_rows(name, rows):
            tile = sb.tile([P, PACK, Q], F32, name=name, tag="raw", bufs=2, align_bytes=64)
            nc.sync.dma_start(out=tile[:], in_=rows.rearrange("(p j) q -> p j q", j=PACK))
            return tile

        def gather(name, window, dtype):
            tile = sb.tile([P, I], dtype, name=name, align_bytes=64)
            nc.vector.tensor_copy(tile[:], window[:].bitcast(dtype).indirect(offsets[:]))
            return tile

        def quantise(name, raw):
            grouped = sb.tile([P, Q, PACK], BF16, name=name + "_bf", tag=name + "_bf", align_bytes=64)
            nc.scalar.copy(
                out=grouped[:].rearrange("p (c i) j -> p c j i", i=4),
                in_=raw[:].rearrange("p j (c i) -> p c j i", i=4),
            )
            codes = sb.tile([P, Q], U32, name=name + "_codes", align_bytes=64)
            scale = sb.tile([P, Q], U8, name=name + "_scale", align_bytes=64)
            nc.vector.quantize_mx(
                out=codes[:].bitcast(FP8X4), scales=scale[:], in_=grouped[:].rearrange("p q j -> p (q j)")
            )
            return codes, scale

        def scores(name, rows, words, scale, row0):
            acc = ps.tile([P, I], F32, name=name)
            nc.tensor.matmul_mx(
                out=acc[:],
                lhsT=rows[0][:].bitcast(FP8X4),
                lhsT_scale=rows[1][:],
                rhs=words[:].bitcast(FP8X4),
                rhs_scale=scale[row0:, :],
                start=True,
                stop=True,
            )
            return acc

        def column(name):
            return sb.tile([P, 1], F32, name=name)

        def by_page(ap):
            return ap.rearrange("p (g j) -> p g j", j=PAGE)

        def spread(tile):
            return tile[:].unsqueeze(2).to_broadcast([P, G, PAGE])

        offsets = sb.tile([P, I // 16], U16, name="offsets")
        nc.sync.dma_start(offsets[:], offs)
        key_words = load_words("key_words", keys_words, "key_words")
        key_scales = load_scales("key_scales", keys_scales, KEY_ROW0, nc.scalar, "key_scales")
        q2_raw = load_rows("q2_raw", query2)
        q1_raw = load_rows("q1_raw", query)
        val_words = load_words("val_words", vals_words, "val_words")
        val_scales = load_scales("val_scales", vals_scales, VAL_ROW0, nc.sync, "val_scales")

        placed = sb.tile([P, T], F32, name="placed")
        nc.vector.memset(placed[:], 0.0)

        ks = gather("ks", key_scales, U8)
        kw = gather("kw", key_words, U32)
        q2 = quantise("q2", q2_raw)
        go_raw = load_rows("go_raw", gout)
        q1 = quantise("q1", q1_raw)
        dq_raw = load_rows("dq_raw", dquery)
        b = scores("b", q2, kw, ks, KEY_ROW0)
        a = scores("a", q1, kw, ks, KEY_ROW0)

        pb = sb.tile([P, I], F32, name="pb")
        nc.scalar.activation(out=pb[:], in_=b[:], func=ACT.Exp)
        pa = sb.tile([P, I], F32, name="pa")
        z = column("z")
        nc.scalar.activation(out=pa[:], in_=a[:], func=ACT.Exp, accum_out=z[:])

        vw = gather("vw", val_words, U32)
        base_sb = sb.tile([P, T], F32, name="base_sb", tag="val_words", align_bytes=64)
        nc.sync.dma_start(out=base_sb[:], in_=base)
        vs = gather("vs", val_scales, U8)
        c0 = scores("c0", quantise("go", go_raw), vw, vs, VAL_ROW0)
        ta = scores("ta", quantise("dq", dq_raw), kw, ks, KEY_ROW0)

        stats = sb.tile([P, G + 1], F32, name="stats", tag="go_bf", align_bytes=64)
        sbp = stats[:, 0:G]
        rz = stats[:, G : G + 1]
        nc.vector.tensor_reduce(out=sbp, in_=by_page(pb[:]), axis=AX.X, op=ALU.add)
        nc.vector.reciprocal(out=rz, in_=z[:])
        root = sb.tile([P, G], F32, name="root")
        nc.scalar.activation(out=root[:], in_=sbp, func=ACT.Abs_reciprocal_sqrt, scale=1.0 / 512.0)
        rsb = sb.tile([P, G], F32, name="rsb")
        nc.scalar.activation(out=rsb[:], in_=root[:], func=ACT.Square)
        nrz = column("nrz")
        nc.scalar.mul(nrz[:], rz, -1.0)


        quads = sb.tile([P, G, 4], F32, name="quads", tag="dq_bf", align_bytes=64)
        nc.gpsimd.tensor_tensor(out=quads[:], in0=by_page(pa[:])[:, :, 0:4], in1=by_page(pa[:])[:, :, 4:8], op=ALU.add)
        pairs = sb.tile([P, G, 2], F32, name="pairs")
        nc.gpsimd.tensor_tensor(out=pairs[:], in0=quads[:, :, 0:2], in1=quads[:, :, 2:4], op=ALU.add)
        pairs_n = sb.tile([P, G, 2], F32, name="pairs_n")
        nc.gpsimd.tensor_scalar(
            out=pairs_n[:], in0=pairs[:], scalar1=rz, scalar2=0.0, op0=ALU.mult, op1=ALU.add
        )
        share = sb.tile([P, G, 2], F32, name="share")
        nc.gpsimd.tensor_tensor(
            out=share[:], in0=pairs_n[:], in1=rsb[:].unsqueeze(2).to_broadcast([P, G, 2]), op=ALU.mult
        )

        drr = sb.tile([P, I], F32, name="drr")
        nc.vector.tensor_tensor(out=drr[:], in0=c0[:], in1=pb[:], op=ALU.mult)
        junk = sb.tile([P, I], F32, name="junk")
        m = column("m")
        nc.vector.scalar_tensor_tensor(
            out=junk[:], in0=pa[:], scalar=rz, in1=ta[:], op0=ALU.mult, op1=ALU.mult, accum_out=m[:]
        )
        dr = sb.tile([P, G], F32, name="dr")
        nc.vector.tensor_reduce(out=dr[:], in_=by_page(drr[:]), axis=AX.X, op=ALU.add)
        e = sb.tile([P, I], F32, name="e")

        def centred(cols):
            nc.vector.scalar_tensor_tensor(
                out=e[:, cols], in0=ta[:, cols], scalar=m[:], in1=pa[:, cols], op0=ALU.subtract, op1=ALU.mult
            )

        centred(slice(0, I // 2))
        u = sb.tile([P, G], F32, name="u")
        nc.vector.scalar_tensor_tensor(
            out=u[:], in0=dr[:], scalar=rz, in1=rsb[:], op0=ALU.mult, op1=ALU.mult
        )
        junk2 = sb.tile([P, G, 2], F32, name="junk2")
        ubar = column("ubar")
        nc.vector.scalar_tensor_tensor(
            out=junk2[:], in0=dr[:].unsqueeze(2).to_broadcast([P, G, 2]), scalar=rz, in1=share[:],
            op0=ALU.mult, op1=ALU.mult, accum_out=ubar[:],
        )
        centred(slice(I // 2, I))
        x = sb.tile([P, I], F32, name="x")
        cz = column("cz")
        nc.vector.scalar_tensor_tensor(
            out=by_page(x[:]), in0=spread(u), scalar=ubar[:], in1=by_page(e[:]),
            op0=ALU.subtract, op1=ALU.mult, accum_out=cz[:],
        )
        y = sb.tile([P, I], F32, name="y")
        nc.vector.tensor_scalar(
            out=y[:], in0=pa[:], scalar1=cz[:], scalar2=nrz[:], op0=ALU.mult, op1=ALU.mult
        )
        nc.vector.tensor_tensor(placed[:].indirect(offsets[:]), x[:], y[:], ALU.add)

        start = 0
        for n, width in enumerate(OUT_CHUNKS):
            cols = slice(start, start + width)
            res = sb.tile([P, width], F32, name="res%d" % n)
            nc.vector.tensor_tensor(out=res[:], in0=placed[:, cols], in1=base_sb[:, cols], op=ALU.add)
            queue = nc.sync if n % 2 == 0 else nc.scalar
            queue.dma_start(out=out[:, cols], in_=res[:])
            start = start + width
